import numpy as np
import ml_dtypes


def mxq(x, axis, fmt="e4m3"):
    dtype, down = {"e4m3": (ml_dtypes.float8_e4m3fn, 7), "e5m2": (ml_dtypes.float8_e5m2, 14)}[fmt]
    v = np.moveaxis(np.asarray(x, np.float32).astype(ml_dtypes.bfloat16).astype(np.float64), axis, -1)
    blocks = v.reshape(v.shape[:-1] + (-1, 32))
    amax = np.abs(blocks).max(-1, keepdims=True)
    byte = np.maximum(np.where(amax > 0, np.frexp(amax)[1] - 1 + 127, 0) - down, 1)
    scale = np.exp2(byte - 127.0)
    codes = (blocks / scale).astype(np.float32).astype(dtype).astype(np.float64)
    return np.moveaxis((codes * scale).reshape(v.shape), -1, axis)


WIDE = False


def mx_kscale(k):
    if not WIDE:
        return np.ones(k)
    levels = np.array([10, -10, 5, -5, 0])
    if k % 512:
        return np.exp2(np.random.permutation(np.resize(levels, k // 32))).repeat(32)
    a = np.empty((k // 512, 16))
    for p in range(k // 512):
        a[p, :8] = np.random.permutation(np.resize(levels, 8))
        for g in range(8):
            far = levels[np.abs(levels - a[p, g]) >= 10]
            a[p, g + 8] = far[np.random.randint(len(far))]
    return np.exp2(a.ravel()).repeat(32)


def f64(x):
    return np.asarray(x).astype(np.float64)


def striped(idx):
    return np.tile(idx.reshape(-1, 16).T, (8, 1)).astype(np.uint16)


def unstriped(offs):
    return offs[:16].T.reshape(-1).astype(np.int64)


E2M1 = np.array([0.0, 0.5, 1.0, 1.5, 2.0, 3.0, 4.0, 6.0, -0.0, -0.5, -1.0, -1.5, -2.0, -3.0, -4.0, -6.0])


def pack_weight(w, fmt):
    k, n = w.shape
    w = f64(np.asarray(w, np.float32).astype(ml_dtypes.bfloat16)).reshape(k // 32, 32, n)
    amax = np.abs(w).max(1)
    if fmt == "e4m3":
        byte = np.frexp(amax)[1] - 1 + 127 - 7
    else:
        mant, ex = np.frexp(amax / 6.0)
        byte = np.where(mant > 0.5, ex, ex - 1) + 127
    byte = np.clip(np.where(amax > 0, byte, 1), 1, 254)
    scaled = (w * np.exp2(127.0 - byte)[:, None, :]).reshape(k, n).astype(np.float32)
    by_word = np.ascontiguousarray(scaled.reshape(k // 512, 128, 4, n).transpose(0, 1, 3, 2))
    if fmt == "e4m3":
        words = by_word.astype(ml_dtypes.float8_e4m3fn).view(np.uint8)
    else:
        c = by_word.astype(ml_dtypes.float4_e2m1fn).view(np.uint8) & 0xF
        words = (c[..., 0::2] | (c[..., 1::2] << 4)).reshape(k // 512, 128, 2 * n)
    return np.ascontiguousarray(words), np.ascontiguousarray(byte.astype(np.uint8).reshape(k // 512, 16, n))


def unpack_weight(words, scales, fmt):
    g, _, n = scales.shape
    words = np.ascontiguousarray(words).reshape(g, 128, n, -1)
    if fmt == "e4m3":
        vals = words.view(ml_dtypes.float8_e4m3fn).astype(np.float64)
    else:
        nib = np.empty((g, 128, n, 4), np.uint8)
        nib[..., 0::2] = words & 0xF
        nib[..., 1::2] = words >> 4
        vals = E2M1[nib]
    vals = vals * np.repeat(np.exp2(scales.astype(np.float64) - 127.0), 8, axis=1)[..., None]
    return vals.transpose(0, 1, 3, 2).reshape(g * 512, n)


def gelu(v):
    return 0.5 * v * (1.0 + np.tanh(np.sqrt(2.0 / np.pi) * (v + 0.044715 * v**3)))


K, T, S, P, P2, H, N = 1024, 4096, 1024, 512, 256, 1024, 512


def setup_inputs():
    n = np.random.standard_normal
    s = mx_kscale(K)[:, None]
    u = mx_kscale(H)[:, None]
    tab_words, tab_scales = pack_weight(n((K, T)) * s, "e4m3")
    w2_words, w2_scales = pack_weight(0.6 * n((H, N)) / (u * u) / np.sqrt(H), "e2m1")
    return {
        "tab_words": tab_words, "tab_scales": tab_scales,
        "offs": striped(np.random.permutation(T)[:S]),
        "pos1": striped(np.random.permutation(S)[:P]),
        "pos2": striped(np.random.permutation(S)[:P]),
        "pos3": striped(np.random.permutation(P)[:P2]),
        "pos4": striped(np.random.permutation(S)[:P2]),
        "w1": (n((K, H)) / s / np.sqrt(K)).astype(np.float32),
        "sheet": (0.7 * n((H, S))).astype(np.float32),
        "gain": (np.exp(0.3 * n(H)) * u[:, 0]).astype(np.float32),
        "w2_words": w2_words, "w2_scales": w2_scales,
        "w3": (0.8 * n((H, N)) / u / np.sqrt(H)).astype(np.float32),
        "go": np.exp(0.4 * n(N)).astype(np.float32),
    }


def reference(tab_words, tab_scales, offs, pos1, pos2, pos3, pos4, w1, sheet, gain,
              w2_words, w2_scales, w3, go):
    v = unpack_weight(tab_words, tab_scales, "e4m3")[:, unstriped(offs)]
    w2 = unpack_weight(w2_words, w2_scales, "e2m1")
    y1 = mxq(f64(w1), 0, "e4m3").T @ v
    h = f64(gain)[:, None] * (y1 + f64(sheet))
    a1 = h[:, unstriped(pos1)] - h[:, unstriped(pos2)]
    card = h[:, unstriped(pos4)]
    a2 = np.maximum(a1[:, unstriped(pos3)], card) * card
    a2q = mxq(a2, 0, "e4m3")
    cardq = mxq(card, 0, "e4m3")
    y2 = w2.T @ a2q + mxq(f64(w3), 0, "e4m3").T @ cardq
    return f64(go)[:, None] * np.tanh(y2)

@@ -1,0 +1,248 @@
+from contextlib import ExitStack
+
+import concourse.mybir as mybir
+
+K, T, S, PAIRS, KEPT, H, N = 1024, 4096, 1024, 512, 256, 1024, 512
+FLOPS = 2 * K * H * S + 2 * 2 * H * N * KEPT
+
+F32 = mybir.dt.float32
+BF16 = mybir.dt.bfloat16
+I32 = mybir.dt.int32
+U32 = mybir.dt.uint32
+U16 = mybir.dt.uint16
+U8 = mybir.dt.uint8
+FP8X4 = mybir.dt.float8_e4m3fn_x4
+FP4X4 = mybir.dt.float4_e2m1fn_x4
+ALU = mybir.AluOpType
+ACT = mybir.ActivationFunctionType
+
+P = 128
+PACK = 4
+PASS = P * PACK
+BANK = 512
+K_PASSES = K // PASS
+R_PASSES = H // PASS
+SLICES = R_PASSES * PACK
+N_TILES = N // P
+
+
+def tile_list_burned_file_scores_kernel(
+    tc, tab_words, tab_scales, offs, pos1, pos2, pos3, pos4, w1, sheet, gain, w2_words, w2_scales, w3, go, out
+):
+    nc = tc.nc
+    with ExitStack() as ctx:
+        held = ctx.enter_context(tc.tile_pool(name="held", bufs=1))
+        ring = ctx.enter_context(tc.tile_pool(name="ring", bufs=2))
+        psum_h = ctx.enter_context(tc.psum_pool(name="psum_h", bufs=2))
+        psum_y = ctx.enter_context(tc.psum_pool(name="psum_y", bufs=1))
+
+        def load_list(src, name):
+            tile = held.tile(list(src.shape), U16, name=name)
+            nc.sync.dma_start(tile[:], src)
+            return tile
+
+        def load_rows(src, name):
+            raw = held.tile([P, PACK, src.shape[1]], F32, name=name)
+            nc.sync.dma_start(out=raw[:], in_=src.rearrange("(p i) c -> p i c", i=PACK))
+            return raw
+
+        def load_table_words(a):
+            words = held.tile([P, T], I32, name=f"table_words{a}")
+            nc.sync.dma_start(out=words[:], in_=tab_words[a].rearrange("p t i -> p (t i)").bitcast(I32))
+            return words
+
+        def load_w1(a, b):
+            return load_rows(w1[a * PASS : (a + 1) * PASS, b * PASS : (b + 1) * PASS], f"w1_raw{a}{b}")
+
+        def load_sheet(s):
+            b, t = divmod(s, PACK)
+            rows = held.tile([P, S], F32, name=f"sheet{s}")
+            nc.sync.dma_start(
+                out=rows[:], in_=sheet[b * PASS : (b + 1) * PASS, :].rearrange("(p t) j -> p t j", t=PACK)[:, t, :]
+            )
+            return rows
+
+        table_scales = held.tile([P, T], U8, name="table_scales")
+        nc.vector.memset(table_scales[:].bitcast(I32), 0)
+        for q in range(4):
+            nc.gpsimd.dma_start(
+                out=table_scales[32 * q : 32 * q + 4 * K_PASSES, :].bitcast(I32),
+                in_=tab_scales[:, 4 * q : 4 * q + 4, :].bitcast(I32),
+            )
+        w2_planes = held.tile([P, R_PASSES * N], U8, name="w2_planes", align_bytes=64)
+        nc.gpsimd.memset(w2_planes[:].bitcast(I32), 0)
+
+        idx = load_list(offs, "idx")
+        table_words = [load_table_words(0)]
+        w1_raw = {(0, 0): load_w1(0, 0)}
+        table_words.append(load_table_words(1))
+        w1_raw[1, 0] = load_w1(1, 0)
+        gains = held.tile([P, R_PASSES, PACK], F32, name="gains")
+        nc.sync.dma_start(out=gains[:], in_=gain.rearrange("(b p t) -> p b t", b=R_PASSES, t=PACK))
+        sheets = [load_sheet(0)]
+        p2 = load_list(pos2, "p2")
+        p4 = load_list(pos4, "p4")
+        p1 = load_list(pos1, "p1")
+        p3 = load_list(pos3, "p3")
+        sheets.append(load_sheet(1))
+        w1_raw[0, 1] = load_w1(0, 1)
+        sheets.append(load_sheet(2))
+        w1_raw[1, 1] = load_w1(1, 1)
+        sheets.append(load_sheet(3))
+        w3_raw = [load_rows(w3[0:PASS, :], "w3_raw0")]
+        sheets.append(load_sheet(4))
+        w2_codes = held.tile([P, R_PASSES, 2 * N], U8, name="w2_codes", align_bytes=64)
+        nc.sync.dma_start(out=w2_codes[:].bitcast(I32), in_=w2_words.rearrange("b p c -> p b c").bitcast(I32))
+        for q in range(4):
+            nc.sync.dma_start(
+                out=w2_planes[32 * q : 32 * q + 4, :].bitcast(I32).rearrange("r (b c) -> r b c", b=R_PASSES),
+                in_=w2_scales[:, 4 * q : 4 * q + 4, :].rearrange("b r c -> r b c").bitcast(I32),
+            )
+        sheets.append(load_sheet(5))
+        w3_raw.append(load_rows(w3[PASS : 2 * PASS, :], "w3_raw1"))
+        sheets.append(load_sheet(6))
+        sheets.append(load_sheet(7))
+        out_gains = held.tile([P, N_TILES], F32, name="out_gains")
+        with nc.allow_non_contiguous_dma(reason="one output gain to a partition"):
+            nc.sync.dma_start(out=out_gains[:], in_=go.rearrange("(c p) -> p c", p=P))
+
+        def quantize(grouped, name):
+            width = grouped.shape[1] // PACK
+            codes = held.tile([P, width], U32, name=f"{name}_codes", align_bytes=64)
+            scales = held.tile([P, width], U8, name=f"{name}_scales", align_bytes=64)
+            nc.vector.quantize_mx(out=codes[:].bitcast(FP8X4), scales=scales[:], in_=grouped[:])
+            return codes, scales
+
+        def group_w1(a, b):
+            grouped = ring.tile([P, PACK * PASS], BF16, name="w1_grouped", align_bytes=64)
+            nc.scalar.copy(
+                out=grouped[:].rearrange("p (t m i) -> p m i t", t=PACK, i=PACK),
+                in_=w1_raw[a, b][:].rearrange("p i (m t) -> p m i t", t=PACK),
+            )
+            return grouped
+
+        def interleave(copy, src, name):
+            width = src.shape[2]
+            grouped = held.tile([P, PACK * width], BF16, name=name, align_bytes=64)
+            copy(
+                out=grouped[:].rearrange("p (c e i) -> p c i e", e=4, i=PACK),
+                in_=src[:].rearrange("p i (c e) -> p c i e", e=4),
+            )
+            return grouped
+
+        def gather_words(a):
+            picked = held.tile([P, S], U32, name=f"picked_words{a}", align_bytes=64)
+            nc.vector.tensor_copy(picked[:], table_words[a][:].bitcast(U32).indirect(idx[:]))
+            return picked
+
+        picked_words = [gather_words(0)]
+        picked_scales = held.tile([P, S], U8, name="picked_scales", align_bytes=64)
+        nc.vector.tensor_copy(picked_scales[:], table_scales[:].indirect(idx[:]))
+        w1_q = {(0, 0): quantize(group_w1(0, 0), "w1_00")}
+        picked_words.append(gather_words(1))
+        w1_q[1, 0] = quantize(group_w1(1, 0), "w1_10")
+
+        def make_h(s):
+            b, t = divmod(s, PACK)
+            gain_col = gains[:, b, t : t + 1]
+            gained_sheet = ring.tile([P, S], F32, name="gained_sheet")
+            nc.scalar.activation(gained_sheet[:], sheets[s][:], ACT.Copy, scale=gain_col)
+            h = ring.tile([P, S], F32, name="h")
+            for half in range(S // BANK):
+                cols = slice(half * BANK, (half + 1) * BANK)
+                y1 = psum_h.tile([P, BANK], F32, name=f"y1_{half}")
+                for a in range(K_PASSES):
+                    codes, scales = w1_q[a, b]
+                    nc.tensor.matmul_mx(
+                        out=y1[:],
+                        lhsT=codes[:, t * P : (t + 1) * P].bitcast(FP8X4),
+                        lhsT_scale=scales[:, t * P : (t + 1) * P],
+                        rhs=picked_words[a][:, cols].bitcast(FP8X4),
+                        rhs_scale=picked_scales[4 * a :, cols],
+                        start=(a == 0),
+                        stop=(a == K_PASSES - 1),
+                    )
+                nc.vector.scalar_tensor_tensor(h[:, cols], y1[:], gain_col, gained_sheet[:, cols], ALU.mult, ALU.add)
+            return h
+
+        cards = [held.tile([P, PACK, KEPT], F32, name=f"cards{b}") for b in range(R_PASSES)]
+        kept = [held.tile([P, PACK, KEPT], F32, name=f"kept{b}") for b in range(R_PASSES)]
+        larger = held.tile([P, PACK, KEPT], F32, name="larger")
+        a2 = [held.tile([P, PACK, KEPT], F32, name=f"a2_{b}") for b in range(R_PASSES)]
+        y2 = [psum_y.tile([P, KEPT], F32, name=f"y2_{c}") for c in range(N_TILES)]
+
+        def take_max(b, ts):
+            nc.vector.tensor_tensor(larger[:, ts, :], kept[b][:, ts, :], cards[b][:, ts, :], ALU.max)
+
+        def take_product(b, ts):
+            nc.vector.tensor_tensor(a2[b][:, ts, :], larger[:, ts, :], cards[b][:, ts, :], ALU.mult)
+
+        def card_passes(b, w3_q, card_q):
+            for c in range(N_TILES):
+                cols = slice(c * P, (c + 1) * P)
+                nc.tensor.matmul_mx(
+                    out=y2[c][:],
+                    lhsT=w3_q[0][:, cols].bitcast(FP8X4),
+                    lhsT_scale=w3_q[1][:, cols],
+                    rhs=card_q[0][:].bitcast(FP8X4),
+                    rhs_scale=card_q[1][:],
+                    start=(b == 0),
+                    stop=False,
+                )
+
+        def pair_passes(b, a2_q):
+            for c in range(N_TILES):
+                nc.tensor.matmul_mx(
+                    out=y2[c][:],
+                    lhsT=w2_codes[:, b, 2 * c * P : 2 * (c + 1) * P].bitcast(FP4X4),
+                    lhsT_scale=w2_planes[:, b * N + c * P : b * N + (c + 1) * P],
+                    rhs=a2_q[0][:].bitcast(FP8X4),
+                    rhs_scale=a2_q[1][:],
+                    start=False,
+                    stop=(b == R_PASSES - 1),
+                )
+
+        w3_q = {}
+        grouped = {}
+        h = make_h(0)
+        for s in range(SLICES):
+            b, t = divmod(s, PACK)
+            second = ring.tile([P, PAIRS], F32, name="second")
+            nc.vector.tensor_copy(second[:], h[:].indirect(p2[:]))
+            if s == 4:
+                take_max(0, slice(0, PACK))
+            if s == 7:
+                take_max(1, slice(0, PACK - 1))
+            nc.vector.tensor_copy(cards[b][:, t, :], h[:].indirect(p4[:]))
+            if t == PACK - 1:
+                grouped["card", b] = interleave(nc.scalar.copy, cards[b], f"card_grouped{b}")
+            if s == 4:
+                take_product(0, slice(0, PACK))
+                grouped["a2", 0] = interleave(nc.scalar.copy, a2[0], "a2_grouped0")
+            if s == 7:
+                take_product(1, slice(0, PACK - 1))
+            a1 = ring.tile([P, PAIRS], F32, name="a1")
+            nc.vector.tensor_tensor(a1[:], h[:].indirect(p1[:]), second[:], ALU.subtract)
+            if s in (1, 2):
+                w1_q[s - 1, 1] = quantize(group_w1(s - 1, 1), f"w1_{s - 1}1")
+            if s in (3, 6):
+                w3_q[s // 4] = quantize(interleave(nc.scalar.copy, w3_raw[s // 4], "w3_grouped"), f"w3_{s // 4}")
+            if s == 4:
+                card_passes(0, w3_q[0], quantize(grouped["card", 0], "card0"))
+            if s == 5:
+                pair_passes(0, quantize(grouped["a2", 0], "a2_0"))
+            if s == 7:
+                card_passes(1, w3_q[1], quantize(grouped["card", 1], "card1"))
+            if s + 1 < SLICES:
+                h = make_h(s + 1)
+            nc.vector.tensor_copy(kept[b][:, t, :], a1[:].indirect(p3[:]))
+        take_max(1, slice(PACK - 1, PACK))
+        take_product(1, slice(PACK - 1, PACK))
+        pair_passes(1, quantize(interleave(nc.vector.tensor_copy, a2[1], "a2_grouped1"), "a2_1"))
+
+        for c in range(N_TILES):
+            squashed = held.tile([P, KEPT], F32, name=f"squashed{c}")
+            nc.scalar.activation(squashed[:], y2[c][:], ACT.Tanh)
+            scores = held.tile([P, KEPT], F32, name=f"scores{c}")
+            nc.vector.tensor_scalar(scores[:], squashed[:], out_gains[:, c : c + 1], None, ALU.mult)
+            nc.sync.dma_start(out=out[c * P : (c + 1) * P, :], in_=scores[:])

@@ -24,6 +24,8 @@ K_PASSES = K // PASS
 R_PASSES = H // PASS
 SLICES = R_PASSES * PACK
 N_TILES = N // P
+HALVES = 2
+HALF = KEPT // HALVES
 
 
 def tile_list_burned_file_scores_kernel(
@@ -33,7 +35,7 @@ def tile_list_burned_file_scores_kernel(
     with ExitStack() as ctx:
         held = ctx.enter_context(tc.tile_pool(name="held", bufs=1))
         ring = ctx.enter_context(tc.tile_pool(name="ring", bufs=2))
-        psum_h = ctx.enter_context(tc.psum_pool(name="psum_h", bufs=2))
+        psum_h = ctx.enter_context(tc.psum_pool(name="psum_h", bufs=3))
         psum_y = ctx.enter_context(tc.psum_pool(name="psum_y", bufs=1))
 
         def load_list(src, name):
@@ -62,23 +64,23 @@ def tile_list_burned_file_scores_kernel(
             )
             return rows
 
-        table_scales = held.tile([P, T], U8, name="table_scales")
+        table_scales = held.tile([P, T], U8, name="table_scales", tag="scales_then_codes", align_bytes=64)
         nc.vector.memset(table_scales[:].bitcast(I32), 0)
-        for q in range(4):
-            nc.gpsimd.dma_start(
-                out=table_scales[32 * q : 32 * q + 4 * K_PASSES, :].bitcast(I32),
-                in_=tab_scales[:, 4 * q : 4 * q + 4, :].bitcast(I32),
-            )
         w2_planes = held.tile([P, R_PASSES * N], U8, name="w2_planes", align_bytes=64)
         nc.gpsimd.memset(w2_planes[:].bitcast(I32), 0)
 
         idx = load_list(offs, "idx")
         table_words = [load_table_words(0)]
+        for q in range(4):
+            nc.sync.dma_start(
+                out=table_scales[32 * q : 32 * q + 4 * K_PASSES, :].bitcast(I32),
+                in_=tab_scales[:, 4 * q : 4 * q + 4, :].bitcast(I32),
+            )
         w1_raw = {(0, 0): load_w1(0, 0)}
         table_words.append(load_table_words(1))
-        w1_raw[1, 0] = load_w1(1, 0)
         gains = held.tile([P, R_PASSES, PACK], F32, name="gains")
         nc.sync.dma_start(out=gains[:], in_=gain.rearrange("(b p t) -> p b t", b=R_PASSES, t=PACK))
+        w1_raw[1, 0] = load_w1(1, 0)
         sheets = [load_sheet(0)]
         p2 = load_list(pos2, "p2")
         p4 = load_list(pos4, "p4")
@@ -106,143 +108,170 @@ def tile_list_burned_file_scores_kernel(
         with nc.allow_non_contiguous_dma(reason="one output gain to a partition"):
             nc.sync.dma_start(out=out_gains[:], in_=go.rearrange("(c p) -> p c", p=P))
 
-        def quantize(grouped, name):
+        def quantize(grouped, name, codes_tag=None):
             width = grouped.shape[1] // PACK
-            codes = held.tile([P, width], U32, name=f"{name}_codes", align_bytes=64)
+            codes = held.tile([P, width], U32, name=f"{name}_codes", tag=codes_tag or f"{name}_codes", align_bytes=64)
             scales = held.tile([P, width], U8, name=f"{name}_scales", align_bytes=64)
             nc.vector.quantize_mx(out=codes[:].bitcast(FP8X4), scales=scales[:], in_=grouped[:])
             return codes, scales
 
-        def group_w1(a, b):
-            grouped = ring.tile([P, PACK * PASS], BF16, name="w1_grouped", align_bytes=64)
-            nc.scalar.copy(
-                out=grouped[:].rearrange("p (t m i) -> p m i t", t=PACK, i=PACK),
-                in_=w1_raw[a, b][:].rearrange("p i (m t) -> p m i t", t=PACK),
-            )
-            return grouped
+        w1_q = {}
 
-        def interleave(copy, src, name):
-            width = src.shape[2]
-            grouped = held.tile([P, PACK * width], BF16, name=name, align_bytes=64)
+        def quantize_w1(copy, a, b, t0, t1, grouped_tag, codes_tag=None):
+            count = t1 - t0
+            grouped = held.tile([P, count * PASS], BF16, name=f"w1_grouped{a}{b}{t0}", tag=grouped_tag, align_bytes=64)
             copy(
-                out=grouped[:].rearrange("p (c e i) -> p c i e", e=4, i=PACK),
-                in_=src[:].rearrange("p i (c e) -> p c i e", e=4),
+                out=grouped[:].rearrange("p (t m i) -> p m i t", t=count, i=PACK),
+                in_=w1_raw[a, b][:].rearrange("p i (m t) -> p m i t", t=PACK)[:, :, :, t0:t1],
             )
+            codes, scales = quantize(grouped, f"w1_{a}{b}{t0}", codes_tag)
+            for t in range(t0, t1):
+                cols = slice((t - t0) * P, (t - t0 + 1) * P)
+                w1_q[a, b, t] = (codes[:, cols], scales[:, cols])
+
+        def woven(tile):
+            return tile[:].rearrange("p (c e i) -> p c i e", e=4, i=PACK)
+
+        def by_runs(src):
+            return src.rearrange("p i (c e) -> p c i e", e=4)
+
+        def interleave(src, name):
+            grouped = held.tile([P, PACK * src.shape[2]], BF16, name=name, align_bytes=64)
+            nc.scalar.copy(out=woven(grouped), in_=by_runs(src[:]))
             return grouped
 
-        def gather_words(a):
-            picked = held.tile([P, S], U32, name=f"picked_words{a}", align_bytes=64)
+        def gather_words(a, tag):
+            picked = held.tile([P, S], U32, name=f"picked_words{a}", tag=tag, align_bytes=64)
             nc.vector.tensor_copy(picked[:], table_words[a][:].bitcast(U32).indirect(idx[:]))
             return picked
 
-        picked_words = [gather_words(0)]
+        picked_words = [gather_words(0, "picked_words0")]
         picked_scales = held.tile([P, S], U8, name="picked_scales", align_bytes=64)
         nc.vector.tensor_copy(picked_scales[:], table_scales[:].indirect(idx[:]))
-        w1_q = {(0, 0): quantize(group_w1(0, 0), "w1_00")}
-        picked_words.append(gather_words(1))
-        w1_q[1, 0] = quantize(group_w1(1, 0), "w1_10")
+        quantize_w1(nc.scalar.copy, 0, 0, 0, PACK, "grouped_then_words", "scales_then_codes")
+        picked_words.append(gather_words(1, "grouped_then_words"))
+        quantize_w1(nc.vector.tensor_copy, 1, 0, 0, 1, "w1_grouped_first")
 
         def make_h(s):
             b, t = divmod(s, PACK)
             gain_col = gains[:, b, t : t + 1]
-            gained_sheet = ring.tile([P, S], F32, name="gained_sheet")
-            nc.scalar.activation(gained_sheet[:], sheets[s][:], ACT.Copy, scale=gain_col)
+            if s == 0:
+                nc.vector.tensor_scalar(sheets[s][:], sheets[s][:], gain_col, None, ALU.mult)
+            else:
+                nc.scalar.activation(sheets[s][:], sheets[s][:], ACT.Copy, scale=gain_col)
             h = ring.tile([P, S], F32, name="h")
             for half in range(S // BANK):
                 cols = slice(half * BANK, (half + 1) * BANK)
                 y1 = psum_h.tile([P, BANK], F32, name=f"y1_{half}")
                 for a in range(K_PASSES):
-                    codes, scales = w1_q[a, b]
+                    codes, scales = w1_q[a, b, t]
                     nc.tensor.matmul_mx(
                         out=y1[:],
-                        lhsT=codes[:, t * P : (t + 1) * P].bitcast(FP8X4),
-                        lhsT_scale=scales[:, t * P : (t + 1) * P],
+                        lhsT=codes.bitcast(FP8X4),
+                        lhsT_scale=scales,
                         rhs=picked_words[a][:, cols].bitcast(FP8X4),
                         rhs_scale=picked_scales[4 * a :, cols],
                         start=(a == 0),
                         stop=(a == K_PASSES - 1),
                     )
-                nc.vector.scalar_tensor_tensor(h[:, cols], y1[:], gain_col, gained_sheet[:, cols], ALU.mult, ALU.add)
+                nc.vector.scalar_tensor_tensor(h[:, cols], y1[:], gain_col, sheets[s][:, cols], ALU.mult, ALU.add)
             return h
 
         cards = [held.tile([P, PACK, KEPT], F32, name=f"cards{b}") for b in range(R_PASSES)]
         kept = [held.tile([P, PACK, KEPT], F32, name=f"kept{b}") for b in range(R_PASSES)]
         larger = held.tile([P, PACK, KEPT], F32, name="larger")
-        a2 = [held.tile([P, PACK, KEPT], F32, name=f"a2_{b}") for b in range(R_PASSES)]
-        y2 = [psum_y.tile([P, KEPT], F32, name=f"y2_{c}") for c in range(N_TILES)]
+        y2 = [psum_y.tile([P, N_TILES, HALF], F32, name=f"y2_{u}") for u in range(HALVES)]
 
-        def take_max(b, ts):
-            nc.vector.tensor_tensor(larger[:, ts, :], kept[b][:, ts, :], cards[b][:, ts, :], ALU.max)
-
-        def take_product(b, ts):
-            nc.vector.tensor_tensor(a2[b][:, ts, :], larger[:, ts, :], cards[b][:, ts, :], ALU.mult)
+        def take_max(b, ts, cols):
+            nc.vector.tensor_tensor(larger[:, ts, cols], kept[b][:, ts, cols], cards[b][:, ts, cols], ALU.max)
 
         def card_passes(b, w3_q, card_q):
-            for c in range(N_TILES):
-                cols = slice(c * P, (c + 1) * P)
-                nc.tensor.matmul_mx(
-                    out=y2[c][:],
-                    lhsT=w3_q[0][:, cols].bitcast(FP8X4),
-                    lhsT_scale=w3_q[1][:, cols],
-                    rhs=card_q[0][:].bitcast(FP8X4),
-                    rhs_scale=card_q[1][:],
-                    start=(b == 0),
-                    stop=False,
-                )
+            for u in range(HALVES):
+                for c in range(N_TILES):
+                    cols = slice(c * P, (c + 1) * P)
+                    nc.tensor.matmul_mx(
+                        out=y2[u][:, c, :],
+                        lhsT=w3_q[0][:, cols].bitcast(FP8X4),
+                        lhsT_scale=w3_q[1][:, cols],
+                        rhs=card_q[0][:, u * HALF : (u + 1) * HALF].bitcast(FP8X4),
+                        rhs_scale=card_q[1][:, u * HALF : (u + 1) * HALF],
+                        start=(b == 0 and c == 0),
+                        stop=False,
+                    )
 
-        def pair_passes(b, a2_q):
+        def pair_passes(b, u, codes, scales):
             for c in range(N_TILES):
                 nc.tensor.matmul_mx(
-                    out=y2[c][:],
+                    out=y2[u][:, c, :],
                     lhsT=w2_codes[:, b, 2 * c * P : 2 * (c + 1) * P].bitcast(FP4X4),
                     lhsT_scale=w2_planes[:, b * N + c * P : b * N + (c + 1) * P],
-                    rhs=a2_q[0][:].bitcast(FP8X4),
-                    rhs_scale=a2_q[1][:],
+                    rhs=codes.bitcast(FP8X4),
+                    rhs_scale=scales,
                     start=False,
-                    stop=(b == R_PASSES - 1),
+                    stop=(b == R_PASSES - 1 and c == N_TILES - 1),
                 )
 
         w3_q = {}
         grouped = {}
+        every = slice(0, KEPT)
+        halves = [slice(u * HALF, (u + 1) * HALF) for u in range(HALVES)]
         h = make_h(0)
+        quantize_w1(nc.scalar.copy, 1, 0, 1, PACK, "w1_grouped_a")
         for s in range(SLICES):
             b, t = divmod(s, PACK)
             second = ring.tile([P, PAIRS], F32, name="second")
             nc.vector.tensor_copy(second[:], h[:].indirect(p2[:]))
             if s == 4:
-                take_max(0, slice(0, PACK))
+                take_max(0, slice(0, PACK), every)
             if s == 7:
-                take_max(1, slice(0, PACK - 1))
+                take_max(1, slice(0, PACK - 1), every)
             nc.vector.tensor_copy(cards[b][:, t, :], h[:].indirect(p4[:]))
             if t == PACK - 1:
-                grouped["card", b] = interleave(nc.scalar.copy, cards[b], f"card_grouped{b}")
+                grouped["card", b] = interleave(cards[b], f"card_grouped{b}")
             if s == 4:
-                take_product(0, slice(0, PACK))
-                grouped["a2", 0] = interleave(nc.scalar.copy, a2[0], "a2_grouped0")
-            if s == 7:
-                take_product(1, slice(0, PACK - 1))
+                a2 = held.tile([P, PACK, KEPT], F32, name="a2")
+                nc.vector.tensor_tensor(a2[:], larger[:], cards[0][:], ALU.mult)
+                grouped["a2", 0] = interleave(a2, "a2_grouped0")
             a1 = ring.tile([P, PAIRS], F32, name="a1")
             nc.vector.tensor_tensor(a1[:], h[:].indirect(p1[:]), second[:], ALU.subtract)
             if s in (1, 2):
-                w1_q[s - 1, 1] = quantize(group_w1(s - 1, 1), f"w1_{s - 1}1")
+                quantize_w1(nc.scalar.copy, s - 1, 1, 0, PACK, ("w1_grouped_b", "w1_grouped_a")[s - 1])
             if s in (3, 6):
-                w3_q[s // 4] = quantize(interleave(nc.scalar.copy, w3_raw[s // 4], "w3_grouped"), f"w3_{s // 4}")
+                w3_q[s // 4] = quantize(interleave(w3_raw[s // 4], "w3_grouped"), f"w3_{s // 4}")
             if s == 4:
                 card_passes(0, w3_q[0], quantize(grouped["card", 0], "card0"))
             if s == 5:
-                pair_passes(0, quantize(grouped["a2", 0], "a2_0"))
-            if s == 7:
-                card_passes(1, w3_q[1], quantize(grouped["card", 1], "card1"))
+                codes, scales = quantize(grouped["a2", 0], "a2_0")
+                for u in range(HALVES):
+                    pair_passes(0, u, codes[:, halves[u]], scales[:, halves[u]])
             if s + 1 < SLICES:
                 h = make_h(s + 1)
-            nc.vector.tensor_copy(kept[b][:, t, :], a1[:].indirect(p3[:]))
-        take_max(1, slice(PACK - 1, PACK))
-        take_product(1, slice(PACK - 1, PACK))
-        pair_passes(1, quantize(interleave(nc.vector.tensor_copy, a2[1], "a2_grouped1"), "a2_1"))
+                nc.vector.tensor_copy(kept[b][:, t, :], a1[:].indirect(p3[:]))
+        card_passes(1, w3_q[1], quantize(grouped["card", 1], "card1"))
+        last = PACK - 1
+        for u in range(HALVES):
+            nc.vector.tensor_copy(kept[1][:, last, halves[u]], a1[:].indirect(p3[:, u * HALF // 16 : (u + 1) * HALF // 16]))
+        for u in range(HALVES):
+            take_max(1, slice(last, PACK), halves[u])
+        a2_last = []
+        for u in range(HALVES):
+            woven_a2 = held.tile([P, PACK * HALF], BF16, name=f"a2_grouped1{u}", align_bytes=64)
+            nc.vector.tensor_tensor(
+                woven(woven_a2), by_runs(larger[:, :, halves[u]]), by_runs(cards[1][:, :, halves[u]]), ALU.mult
+            )
+            a2_last.append(woven_a2)
+        for u in range(HALVES):
+            codes, scales = quantize(a2_last[u], f"a2_1{u}")
+            pair_passes(1, u, codes[:], scales[:])
 
-        for c in range(N_TILES):
-            squashed = held.tile([P, KEPT], F32, name=f"squashed{c}")
-            nc.scalar.activation(squashed[:], y2[c][:], ACT.Tanh)
-            scores = held.tile([P, KEPT], F32, name=f"scores{c}")
-            nc.vector.tensor_scalar(scores[:], squashed[:], out_gains[:, c : c + 1], None, ALU.mult)
-            nc.sync.dma_start(out=out[c * P : (c + 1) * P, :], in_=scores[:])
+        out_rows = out.rearrange("(c p) j -> p c j", p=P)
+        for u in range(HALVES):
+            for c0 in range(0, N_TILES, 2):
+                tiles = slice(c0, c0 + 2)
+                squashed = held.tile([P, 2, HALF], F32, name=f"squashed{u}{c0}")
+                nc.scalar.activation(squashed[:], y2[u][:, tiles, :], ACT.Tanh)
+                scores = held.tile([P, 2, HALF], F32, name=f"scores{u}{c0}")
+                nc.vector.tensor_tensor(
+                    scores[:], squashed[:], out_gains[:, tiles].unsqueeze(2).to_broadcast([P, 2, HALF]), ALU.mult
+                )
+                nc.sync.dma_start(out=out_rows[:, tiles, halves[u]], in_=scores[:])

@@ -64,6 +64,12 @@ def tile_list_burned_file_scores_kernel(
             )
             return rows
 
+        def load_table_scales(q, a0, a1):
+            nc.sync.dma_start(
+                out=table_scales[32 * q + 4 * a0 : 32 * q + 4 * a1, :].bitcast(I32),
+                in_=tab_scales[a0:a1, 4 * q : 4 * q + 4, :].bitcast(I32),
+            )
+
         table_scales = held.tile([P, T], U8, name="table_scales", tag="scales_then_codes", align_bytes=64)
         nc.vector.memset(table_scales[:].bitcast(I32), 0)
         w2_planes = held.tile([P, R_PASSES * N], U8, name="w2_planes", align_bytes=64)
@@ -71,11 +77,11 @@ def tile_list_burned_file_scores_kernel(
 
         idx = load_list(offs, "idx")
         table_words = [load_table_words(0)]
-        for q in range(4):
-            nc.sync.dma_start(
-                out=table_scales[32 * q : 32 * q + 4 * K_PASSES, :].bitcast(I32),
-                in_=tab_scales[:, 4 * q : 4 * q + 4, :].bitcast(I32),
-            )
+        for q in (0, 2):
+            load_table_scales(q, 0, K_PASSES)
+        for q in (1, 3):
+            for a in range(K_PASSES):
+                load_table_scales(q, a, a + 1)
         w1_raw = {(0, 0): load_w1(0, 0)}
         table_words.append(load_table_words(1))
         gains = held.tile([P, R_PASSES, PACK], F32, name="gains")
@@ -91,8 +97,8 @@ def tile_list_burned_file_scores_kernel(
         sheets.append(load_sheet(2))
         w1_raw[1, 1] = load_w1(1, 1)
         sheets.append(load_sheet(3))
-        w3_raw = [load_rows(w3[0:PASS, :], "w3_raw0")]
-        sheets.append(load_sheet(4))
+        sheets.extend(load_sheet(s) for s in range(4, SLICES))
+        w3_raw = [load_rows(w3[b * PASS : (b + 1) * PASS, :], f"w3_raw{b}") for b in range(R_PASSES)]
         w2_codes = held.tile([P, R_PASSES, 2 * N], U8, name="w2_codes", align_bytes=64)
         nc.sync.dma_start(out=w2_codes[:].bitcast(I32), in_=w2_words.rearrange("b p c -> p b c").bitcast(I32))
         for q in range(4):
@@ -100,10 +106,6 @@ def tile_list_burned_file_scores_kernel(
                 out=w2_planes[32 * q : 32 * q + 4, :].bitcast(I32).rearrange("r (b c) -> r b c", b=R_PASSES),
                 in_=w2_scales[:, 4 * q : 4 * q + 4, :].rearrange("b r c -> r b c").bitcast(I32),
             )
-        sheets.append(load_sheet(5))
-        w3_raw.append(load_rows(w3[PASS : 2 * PASS, :], "w3_raw1"))
-        sheets.append(load_sheet(6))
-        sheets.append(load_sheet(7))
         out_gains = held.tile([P, N_TILES], F32, name="out_gains")
         with nc.allow_non_contiguous_dma(reason="one output gain to a partition"):
             nc.sync.dma_start(out=out_gains[:], in_=go.rearrange("(c p) -> p c", p=P))
@@ -135,8 +137,8 @@ def tile_list_burned_file_scores_kernel(
         def by_runs(src):
             return src.rearrange("p i (c e) -> p c i e", e=4)
 
-        def interleave(src, name):
-            grouped = held.tile([P, PACK * src.shape[2]], BF16, name=name, align_bytes=64)
+        def interleave(src, name, tag):
+            grouped = held.tile([P, PACK * src.shape[2]], BF16, name=name, tag=tag, align_bytes=64)
             nc.scalar.copy(out=woven(grouped), in_=by_runs(src[:]))
             return grouped
 
@@ -174,16 +176,21 @@ def tile_list_burned_file_scores_kernel(
                         start=(a == 0),
                         stop=(a == K_PASSES - 1),
                     )
-                nc.vector.scalar_tensor_tensor(h[:, cols], y1[:], gain_col, sheets[s][:, cols], ALU.mult, ALU.add)
+                if s < 2 or half == 0:
+                    nc.vector.scalar_tensor_tensor(h[:, cols], y1[:], gain_col, sheets[s][:, cols], ALU.mult, ALU.add)
+                else:
+                    gained = held.tile([P, BANK], F32, name=f"gained{s}", tag=f"gained{s}", align_bytes=64)
+                    nc.scalar.activation(gained[:], y1[:], ACT.Copy, scale=gain_col)
+                    nc.gpsimd.tensor_tensor(h[:, cols], gained[:], sheets[s][:, cols], ALU.add)
             return h
 
         cards = [held.tile([P, PACK, KEPT], F32, name=f"cards{b}") for b in range(R_PASSES)]
         kept = [held.tile([P, PACK, KEPT], F32, name=f"kept{b}") for b in range(R_PASSES)]
-        larger = held.tile([P, PACK, KEPT], F32, name="larger")
+        larger = {}
         y2 = [psum_y.tile([P, N_TILES, HALF], F32, name=f"y2_{u}") for u in range(HALVES)]
 
         def take_max(b, ts, cols):
-            nc.vector.tensor_tensor(larger[:, ts, cols], kept[b][:, ts, cols], cards[b][:, ts, cols], ALU.max)
+            nc.vector.tensor_tensor(larger[b][:, ts, cols], kept[b][:, ts, cols], cards[b][:, ts, cols], ALU.max)
 
         def card_passes(b, w3_q, card_q):
             for u in range(HALVES):
@@ -215,38 +222,45 @@ def tile_list_burned_file_scores_kernel(
         grouped = {}
         every = slice(0, KEPT)
         halves = [slice(u * HALF, (u + 1) * HALF) for u in range(HALVES)]
-        h = make_h(0)
+        hs = [make_h(0)]
         quantize_w1(nc.scalar.copy, 1, 0, 1, PACK, "w1_grouped_a")
+        hs.append(make_h(1))
         for s in range(SLICES):
             b, t = divmod(s, PACK)
+            h = hs[s]
             second = ring.tile([P, PAIRS], F32, name="second")
             nc.vector.tensor_copy(second[:], h[:].indirect(p2[:]))
-            if s == 4:
+            if s == 6:
+                larger[0] = held.tile([P, PACK, KEPT], F32, name="larger0", tag="gained7", align_bytes=64)
                 take_max(0, slice(0, PACK), every)
             if s == 7:
+                larger[1] = held.tile([P, PACK, KEPT], F32, name="larger1", tag="gained7", align_bytes=64)
                 take_max(1, slice(0, PACK - 1), every)
             nc.vector.tensor_copy(cards[b][:, t, :], h[:].indirect(p4[:]))
-            if t == PACK - 1:
-                grouped["card", b] = interleave(cards[b], f"card_grouped{b}")
-            if s == 4:
+            if s == 7:
+                grouped["card", 1] = interleave(cards[1], "card_grouped1", "card_grouped1")
+            if s == 6:
                 a2 = held.tile([P, PACK, KEPT], F32, name="a2")
-                nc.vector.tensor_tensor(a2[:], larger[:], cards[0][:], ALU.mult)
-                grouped["a2", 0] = interleave(a2, "a2_grouped0")
+                nc.vector.tensor_tensor(a2[:], larger[0][:], cards[0][:], ALU.mult)
+                grouped["a2", 0] = interleave(a2, "a2_grouped0", "a2_grouped0")
             a1 = ring.tile([P, PAIRS], F32, name="a1")
             nc.vector.tensor_tensor(a1[:], h[:].indirect(p1[:]), second[:], ALU.subtract)
-            if s in (1, 2):
-                quantize_w1(nc.scalar.copy, s - 1, 1, 0, PACK, ("w1_grouped_b", "w1_grouped_a")[s - 1])
-            if s in (3, 6):
-                w3_q[s // 4] = quantize(interleave(w3_raw[s // 4], "w3_grouped"), f"w3_{s // 4}")
-            if s == 4:
-                card_passes(0, w3_q[0], quantize(grouped["card", 0], "card0"))
+            if s + 2 < SLICES:
+                hs.append(make_h(s + 2))
+            if s + 1 < SLICES:
+                nc.vector.tensor_copy(kept[b][:, t, :], a1[:].indirect(p3[:]))
+            if s in (0, 1):
+                quantize_w1(nc.scalar.copy, s, 1, 0, PACK, ("w1_grouped_b", "w1_grouped_a")[s])
             if s == 5:
+                grouped["card", 0] = interleave(cards[0], "card_grouped0", "gained6")
+                for c in range(R_PASSES):
+                    tag = ("w1_grouped_b", "w1_grouped_a")[c]
+                    w3_q[c] = quantize(interleave(w3_raw[c], f"w3_grouped{c}", tag), f"w3_{c}")
+                card_passes(0, w3_q[0], quantize(grouped["card", 0], "card0"))
+            if s == 6:
                 codes, scales = quantize(grouped["a2", 0], "a2_0")
                 for u in range(HALVES):
                     pair_passes(0, u, codes[:, halves[u]], scales[:, halves[u]])
-            if s + 1 < SLICES:
-                h = make_h(s + 1)
-                nc.vector.tensor_copy(kept[b][:, t, :], a1[:].indirect(p3[:]))
         card_passes(1, w3_q[1], quantize(grouped["card", 1], "card1"))
         last = PACK - 1
         for u in range(HALVES):
@@ -257,7 +271,7 @@ def tile_list_burned_file_scores_kernel(
         for u in range(HALVES):
             woven_a2 = held.tile([P, PACK * HALF], BF16, name=f"a2_grouped1{u}", align_bytes=64)
             nc.vector.tensor_tensor(
-                woven(woven_a2), by_runs(larger[:, :, halves[u]]), by_runs(cards[1][:, :, halves[u]]), ALU.mult
+                woven(woven_a2), by_runs(larger[1][:, :, halves[u]]), by_runs(cards[1][:, :, halves[u]]), ALU.mult
             )
             a2_last.append(woven_a2)
         for u in range(HALVES):

@@ -26,6 +26,8 @@ SLICES = R_PASSES * PACK
 N_TILES = N // P
 HALVES = 2
 HALF = KEPT // HALVES
+VECTOR_COLS = 128
+FIRST_SHARED = 2
 
 
 def tile_list_burned_file_scores_kernel(
@@ -58,7 +60,7 @@ def tile_list_burned_file_scores_kernel(
 
         def load_sheet(s):
             b, t = divmod(s, PACK)
-            rows = held.tile([P, S], F32, name=f"sheet{s}")
+            rows = held.tile([P, S], F32, name=f"sheet{s}", tag=f"sheet{s}", align_bytes=64)
             nc.sync.dma_start(
                 out=rows[:], in_=sheet[b * PASS : (b + 1) * PASS, :].rearrange("(p t) j -> p t j", t=PACK)[:, t, :]
             )
@@ -92,12 +94,10 @@ def tile_list_burned_file_scores_kernel(
         p4 = load_list(pos4, "p4")
         p1 = load_list(pos1, "p1")
         p3 = load_list(pos3, "p3")
-        sheets.append(load_sheet(1))
+        sheets.extend(load_sheet(s) for s in range(1, 3))
         w1_raw[0, 1] = load_w1(0, 1)
-        sheets.append(load_sheet(2))
         w1_raw[1, 1] = load_w1(1, 1)
-        sheets.append(load_sheet(3))
-        sheets.extend(load_sheet(s) for s in range(4, SLICES))
+        sheets.extend(load_sheet(s) for s in range(3, SLICES))
         w3_raw = [load_rows(w3[b * PASS : (b + 1) * PASS, :], f"w3_raw{b}") for b in range(R_PASSES)]
         w2_codes = held.tile([P, R_PASSES, 2 * N], U8, name="w2_codes", align_bytes=64)
         nc.sync.dma_start(out=w2_codes[:].bitcast(I32), in_=w2_words.rearrange("b p c -> p b c").bitcast(I32))
@@ -162,6 +162,8 @@ def tile_list_burned_file_scores_kernel(
             else:
                 nc.scalar.activation(sheets[s][:], sheets[s][:], ACT.Copy, scale=gain_col)
             h = ring.tile([P, S], F32, name="h")
+            if s >= FIRST_SHARED:
+                gained = held.tile([P, S - VECTOR_COLS], F32, name=f"gained{s}", tag=f"gained{s}")
             for half in range(S // BANK):
                 cols = slice(half * BANK, (half + 1) * BANK)
                 y1 = psum_h.tile([P, BANK], F32, name=f"y1_{half}")
@@ -176,12 +178,22 @@ def tile_list_burned_file_scores_kernel(
                         start=(a == 0),
                         stop=(a == K_PASSES - 1),
                     )
-                if s < 2 or half == 0:
-                    nc.vector.scalar_tensor_tensor(h[:, cols], y1[:], gain_col, sheets[s][:, cols], ALU.mult, ALU.add)
-                else:
-                    gained = held.tile([P, BANK], F32, name=f"gained{s}", tag=f"gained{s}", align_bytes=64)
-                    nc.scalar.activation(gained[:], y1[:], ACT.Copy, scale=gain_col)
-                    nc.gpsimd.tensor_tensor(h[:, cols], gained[:], sheets[s][:, cols], ALU.add)
+                on_vector = BANK if s < FIRST_SHARED else (VECTOR_COLS if half == 0 else 0)
+                lo = half * BANK
+                if on_vector < BANK:
+                    nc.scalar.activation(
+                        gained[:, lo + on_vector - VECTOR_COLS : lo + BANK - VECTOR_COLS],
+                        y1[:, on_vector:],
+                        ACT.Copy,
+                        scale=gain_col,
+                    )
+                if on_vector:
+                    part = slice(lo, lo + on_vector)
+                    nc.vector.scalar_tensor_tensor(
+                        h[:, part], y1[:, :on_vector], gain_col, sheets[s][:, part], ALU.mult, ALU.add
+                    )
+            if s >= FIRST_SHARED:
+                nc.gpsimd.tensor_tensor(h[:, VECTOR_COLS:], gained[:], sheets[s][:, VECTOR_COLS:], ALU.add)
             return h
 
         cards = [held.tile([P, PACK, KEPT], F32, name=f"cards{b}") for b in range(R_PASSES)]
@@ -219,6 +231,7 @@ def tile_list_burned_file_scores_kernel(
                 )
 
         w3_q = {}
+        a1 = {}
         grouped = {}
         every = slice(0, KEPT)
         halves = [slice(u * HALF, (u + 1) * HALF) for u in range(HALVES)]
@@ -231,28 +244,30 @@ def tile_list_burned_file_scores_kernel(
             second = ring.tile([P, PAIRS], F32, name="second")
             nc.vector.tensor_copy(second[:], h[:].indirect(p2[:]))
             if s == 6:
-                larger[0] = held.tile([P, PACK, KEPT], F32, name="larger0", tag="gained7", align_bytes=64)
+                larger[0] = held.tile([P, PACK, KEPT], F32, name="larger0", tag="sheet7", align_bytes=64)
                 take_max(0, slice(0, PACK), every)
-            if s == 7:
-                larger[1] = held.tile([P, PACK, KEPT], F32, name="larger1", tag="gained7", align_bytes=64)
-                take_max(1, slice(0, PACK - 1), every)
+            if s == 2:
+                first = held.tile([P, PAIRS], F32, name="first_held", tag="w1_grouped_a", align_bytes=64)
+            else:
+                first = ring.tile([P, PAIRS], F32, name="first")
+            nc.vector.tensor_copy(first[:], h[:].indirect(p1[:]))
+            a1[s] = held.tile([P, PAIRS], F32, name=f"a1_{s}", tag=f"gained{s + 1}")
+            nc.gpsimd.tensor_tensor(a1[s][:], first[:], second[:], ALU.subtract)
             nc.vector.tensor_copy(cards[b][:, t, :], h[:].indirect(p4[:]))
             if s == 7:
                 grouped["card", 1] = interleave(cards[1], "card_grouped1", "card_grouped1")
             if s == 6:
                 a2 = held.tile([P, PACK, KEPT], F32, name="a2")
-                nc.vector.tensor_tensor(a2[:], larger[0][:], cards[0][:], ALU.mult)
+                nc.gpsimd.tensor_tensor(a2[:], larger[0][:], cards[0][:], ALU.mult)
                 grouped["a2", 0] = interleave(a2, "a2_grouped0", "a2_grouped0")
-            a1 = ring.tile([P, PAIRS], F32, name="a1")
-            nc.vector.tensor_tensor(a1[:], h[:].indirect(p1[:]), second[:], ALU.subtract)
             if s + 2 < SLICES:
                 hs.append(make_h(s + 2))
-            if s + 1 < SLICES:
-                nc.vector.tensor_copy(kept[b][:, t, :], a1[:].indirect(p3[:]))
+            if s > 0:
+                nc.vector.tensor_copy(kept[(s - 1) // PACK][:, (s - 1) % PACK, :], a1[s - 1][:].indirect(p3[:]))
             if s in (0, 1):
                 quantize_w1(nc.scalar.copy, s, 1, 0, PACK, ("w1_grouped_b", "w1_grouped_a")[s])
             if s == 5:
-                grouped["card", 0] = interleave(cards[0], "card_grouped0", "gained6")
+                grouped["card", 0] = interleave(cards[0], "card_grouped0", "sheet6")
                 for c in range(R_PASSES):
                     tag = ("w1_grouped_b", "w1_grouped_a")[c]
                     w3_q[c] = quantize(interleave(w3_raw[c], f"w3_grouped{c}", tag), f"w3_{c}")
@@ -261,10 +276,12 @@ def tile_list_burned_file_scores_kernel(
                 codes, scales = quantize(grouped["a2", 0], "a2_0")
                 for u in range(HALVES):
                     pair_passes(0, u, codes[:, halves[u]], scales[:, halves[u]])
+        larger[1] = held.tile([P, PACK, KEPT], F32, name="larger1", tag="sheet7", align_bytes=64)
+        take_max(1, slice(0, PACK - 1), every)
         card_passes(1, w3_q[1], quantize(grouped["card", 1], "card1"))
         last = PACK - 1
         for u in range(HALVES):
-            nc.vector.tensor_copy(kept[1][:, last, halves[u]], a1[:].indirect(p3[:, u * HALF // 16 : (u + 1) * HALF // 16]))
+            nc.vector.tensor_copy(kept[1][:, last, halves[u]], a1[SLICES - 1][:].indirect(p3[:, u * HALF // 16 : (u + 1) * HALF // 16]))
         for u in range(HALVES):
             take_max(1, slice(last, PACK), halves[u])
         a2_last = []

from contextlib import ExitStack

import concourse.mybir as mybir

K, T, S, PAIRS, KEPT, H, N = 1024, 4096, 1024, 512, 256, 1024, 512
FLOPS = 2 * K * H * S + 2 * 2 * H * N * KEPT

F32 = mybir.dt.float32
BF16 = mybir.dt.bfloat16
I32 = mybir.dt.int32
U32 = mybir.dt.uint32
U16 = mybir.dt.uint16
U8 = mybir.dt.uint8
FP8X4 = mybir.dt.float8_e4m3fn_x4
FP4X4 = mybir.dt.float4_e2m1fn_x4
ALU = mybir.AluOpType
ACT = mybir.ActivationFunctionType

P = 128
PACK = 4
PASS = P * PACK
BANK = 512
K_PASSES = K // PASS
R_PASSES = H // PASS
SLICES = R_PASSES * PACK
N_TILES = N // P
HALVES = 2
HALF = KEPT // HALVES
VECTOR_COLS = 128
FIRST_SHARED = 2


def tile_list_burned_file_scores_kernel(
    tc, tab_words, tab_scales, offs, pos1, pos2, pos3, pos4, w1, sheet, gain, w2_words, w2_scales, w3, go, out
):
    nc = tc.nc
    with ExitStack() as ctx:
        held = ctx.enter_context(tc.tile_pool(name="held", bufs=1))
        ring = ctx.enter_context(tc.tile_pool(name="ring", bufs=2))
        psum_h = ctx.enter_context(tc.psum_pool(name="psum_h", bufs=3))
        psum_y = ctx.enter_context(tc.psum_pool(name="psum_y", bufs=1))

        def load_list(src, name):
            tile = held.tile(list(src.shape), U16, name=name)
            nc.sync.dma_start(tile[:], src)
            return tile

        def load_rows(src, name):
            raw = held.tile([P, PACK, src.shape[1]], F32, name=name)
            nc.sync.dma_start(out=raw[:], in_=src.rearrange("(p i) c -> p i c", i=PACK))
            return raw

        def load_table_words(a):
            words = held.tile([P, T], I32, name=f"table_words{a}")
            nc.sync.dma_start(out=words[:], in_=tab_words[a].rearrange("p t i -> p (t i)").bitcast(I32))
            return words

        def load_w1(a, b):
            return load_rows(w1[a * PASS : (a + 1) * PASS, b * PASS : (b + 1) * PASS], f"w1_raw{a}{b}")

        def load_sheet(s):
            b, t = divmod(s, PACK)
            rows = held.tile([P, S], F32, name=f"sheet{s}", tag=f"sheet{s}", align_bytes=64)
            nc.sync.dma_start(
                out=rows[:], in_=sheet[b * PASS : (b + 1) * PASS, :].rearrange("(p t) j -> p t j", t=PACK)[:, t, :]
            )
            return rows

        def load_table_scales(q, a0, a1):
            nc.sync.dma_start(
                out=table_scales[32 * q + 4 * a0 : 32 * q + 4 * a1, :].bitcast(I32),
                in_=tab_scales[a0:a1, 4 * q : 4 * q + 4, :].bitcast(I32),
            )

        table_scales = held.tile([P, T], U8, name="table_scales", tag="scales_then_codes", align_bytes=64)
        nc.vector.memset(table_scales[:].bitcast(I32), 0)
        w2_planes = held.tile([P, R_PASSES * N], U8, name="w2_planes", align_bytes=64)
        nc.gpsimd.memset(w2_planes[:].bitcast(I32), 0)

        idx = load_list(offs, "idx")
        table_words = [load_table_words(0)]
        for q in (0, 2):
            load_table_scales(q, 0, K_PASSES)
        for q in (1, 3):
            for a in range(K_PASSES):
                load_table_scales(q, a, a + 1)
        w1_raw = {(0, 0): load_w1(0, 0)}
        table_words.append(load_table_words(1))
        gains = held.tile([P, R_PASSES, PACK], F32, name="gains")
        nc.sync.dma_start(out=gains[:], in_=gain.rearrange("(b p t) -> p b t", b=R_PASSES, t=PACK))
        w1_raw[1, 0] = load_w1(1, 0)
        sheets = [load_sheet(0)]
        p2 = load_list(pos2, "p2")
        p4 = load_list(pos4, "p4")
        p1 = load_list(pos1, "p1")
        p3 = load_list(pos3, "p3")
        sheets.extend(load_sheet(s) for s in range(1, 3))
        w1_raw[0, 1] = load_w1(0, 1)
        w1_raw[1, 1] = load_w1(1, 1)
        sheets.extend(load_sheet(s) for s in range(3, SLICES))
        w3_raw = [load_rows(w3[b * PASS : (b + 1) * PASS, :], f"w3_raw{b}") for b in range(R_PASSES)]
        w2_codes = held.tile([P, R_PASSES, 2 * N], U8, name="w2_codes", align_bytes=64)
        nc.sync.dma_start(out=w2_codes[:].bitcast(I32), in_=w2_words.rearrange("b p c -> p b c").bitcast(I32))
        for q in range(4):
            nc.sync.dma_start(
                out=w2_planes[32 * q : 32 * q + 4, :].bitcast(I32).rearrange("r (b c) -> r b c", b=R_PASSES),
                in_=w2_scales[:, 4 * q : 4 * q + 4, :].rearrange("b r c -> r b c").bitcast(I32),
            )
        out_gains = held.tile([P, N_TILES], F32, name="out_gains")
        with nc.allow_non_contiguous_dma(reason="one output gain to a partition"):
            nc.sync.dma_start(out=out_gains[:], in_=go.rearrange("(c p) -> p c", p=P))

        def quantize(grouped, name, codes_tag=None):
            width = grouped.shape[1] // PACK
            codes = held.tile([P, width], U32, name=f"{name}_codes", tag=codes_tag or f"{name}_codes", align_bytes=64)
            scales = held.tile([P, width], U8, name=f"{name}_scales", align_bytes=64)
            nc.vector.quantize_mx(out=codes[:].bitcast(FP8X4), scales=scales[:], in_=grouped[:])
            return codes, scales

        w1_q = {}

        def quantize_w1(copy, a, b, t0, t1, grouped_tag, codes_tag=None):
            count = t1 - t0
            grouped = held.tile([P, count * PASS], BF16, name=f"w1_grouped{a}{b}{t0}", tag=grouped_tag, align_bytes=64)
            copy(
                out=grouped[:].rearrange("p (t m i) -> p m i t", t=count, i=PACK),
                in_=w1_raw[a, b][:].rearrange("p i (m t) -> p m i t", t=PACK)[:, :, :, t0:t1],
            )
            codes, scales = quantize(grouped, f"w1_{a}{b}{t0}", codes_tag)
            for t in range(t0, t1):
                cols = slice((t - t0) * P, (t - t0 + 1) * P)
                w1_q[a, b, t] = (codes[:, cols], scales[:, cols])

        def woven(tile):
            return tile[:].rearrange("p (c e i) -> p c i e", e=4, i=PACK)

        def by_runs(src):
            return src.rearrange("p i (c e) -> p c i e", e=4)

        def interleave(src, name, tag):
            grouped = held.tile([P, PACK * src.shape[2]], BF16, name=name, tag=tag, align_bytes=64)
            nc.scalar.copy(out=woven(grouped), in_=by_runs(src[:]))
            return grouped

        def gather_words(a, tag):
            picked = held.tile([P, S], U32, name=f"picked_words{a}", tag=tag, align_bytes=64)
            nc.vector.tensor_copy(picked[:], table_words[a][:].bitcast(U32).indirect(idx[:]))
            return picked

        picked_words = [gather_words(0, "picked_words0")]
        picked_scales = held.tile([P, S], U8, name="picked_scales", align_bytes=64)
        nc.vector.tensor_copy(picked_scales[:], table_scales[:].indirect(idx[:]))
        quantize_w1(nc.scalar.copy, 0, 0, 0, PACK, "grouped_then_words", "scales_then_codes")
        picked_words.append(gather_words(1, "grouped_then_words"))
        quantize_w1(nc.vector.tensor_copy, 1, 0, 0, 1, "w1_grouped_first")

        def make_h(s):
            b, t = divmod(s, PACK)
            gain_col = gains[:, b, t : t + 1]
            if s == 0:
                nc.vector.tensor_scalar(sheets[s][:], sheets[s][:], gain_col, None, ALU.mult)
            else:
                nc.scalar.activation(sheets[s][:], sheets[s][:], ACT.Copy, scale=gain_col)
            h = ring.tile([P, S], F32, name="h")
            if s >= FIRST_SHARED:
                gained = held.tile([P, S - VECTOR_COLS], F32, name=f"gained{s}", tag=f"gained{s}")
            for half in range(S // BANK):
                cols = slice(half * BANK, (half + 1) * BANK)
                y1 = psum_h.tile([P, BANK], F32, name=f"y1_{half}")
                for a in range(K_PASSES):
                    codes, scales = w1_q[a, b, t]
                    nc.tensor.matmul_mx(
                        out=y1[:],
                        lhsT=codes.bitcast(FP8X4),
                        lhsT_scale=scales,
                        rhs=picked_words[a][:, cols].bitcast(FP8X4),
                        rhs_scale=picked_scales[4 * a :, cols],
                        start=(a == 0),
                        stop=(a == K_PASSES - 1),
                    )
                on_vector = BANK if s < FIRST_SHARED else (VECTOR_COLS if half == 0 else 0)
                lo = half * BANK
                if on_vector < BANK:
                    nc.scalar.activation(
                        gained[:, lo + on_vector - VECTOR_COLS : lo + BANK - VECTOR_COLS],
                        y1[:, on_vector:],
                        ACT.Copy,
                        scale=gain_col,
                    )
                if on_vector:
                    part = slice(lo, lo + on_vector)
                    nc.vector.scalar_tensor_tensor(
                        h[:, part], y1[:, :on_vector], gain_col, sheets[s][:, part], ALU.mult, ALU.add
                    )
            if s >= FIRST_SHARED:
                nc.gpsimd.tensor_tensor(h[:, VECTOR_COLS:], gained[:], sheets[s][:, VECTOR_COLS:], ALU.add)
            return h

        cards = [held.tile([P, PACK, KEPT], F32, name=f"cards{b}") for b in range(R_PASSES)]
        kept = [held.tile([P, PACK, KEPT], F32, name=f"kept{b}") for b in range(R_PASSES)]
        larger = {}
        y2 = [psum_y.tile([P, N_TILES, HALF], F32, name=f"y2_{u}") for u in range(HALVES)]

        def take_max(b, ts, cols):
            nc.vector.tensor_tensor(larger[b][:, ts, cols], kept[b][:, ts, cols], cards[b][:, ts, cols], ALU.max)

        def card_passes(b, w3_q, card_q):
            for u in range(HALVES):
                for c in range(N_TILES):
                    cols = slice(c * P, (c + 1) * P)
                    nc.tensor.matmul_mx(
                        out=y2[u][:, c, :],
                        lhsT=w3_q[0][:, cols].bitcast(FP8X4),
                        lhsT_scale=w3_q[1][:, cols],
                        rhs=card_q[0][:, u * HALF : (u + 1) * HALF].bitcast(FP8X4),
                        rhs_scale=card_q[1][:, u * HALF : (u + 1) * HALF],
                        start=(b == 0 and c == 0),
                        stop=False,
                    )

        def pair_passes(b, u, codes, scales):
            for c in range(N_TILES):
                nc.tensor.matmul_mx(
                    out=y2[u][:, c, :],
                    lhsT=w2_codes[:, b, 2 * c * P : 2 * (c + 1) * P].bitcast(FP4X4),
                    lhsT_scale=w2_planes[:, b * N + c * P : b * N + (c + 1) * P],
                    rhs=codes.bitcast(FP8X4),
                    rhs_scale=scales,
                    start=False,
                    stop=(b == R_PASSES - 1 and c == N_TILES - 1),
                )

        w3_q = {}
        a1 = {}
        grouped = {}
        every = slice(0, KEPT)
        halves = [slice(u * HALF, (u + 1) * HALF) for u in range(HALVES)]
        hs = [make_h(0)]
        quantize_w1(nc.scalar.copy, 1, 0, 1, PACK, "w1_grouped_a")
        hs.append(make_h(1))
        for s in range(SLICES):
            b, t = divmod(s, PACK)
            h = hs[s]
            second = ring.tile([P, PAIRS], F32, name="second")
            nc.vector.tensor_copy(second[:], h[:].indirect(p2[:]))
            if s == 6:
                larger[0] = held.tile([P, PACK, KEPT], F32, name="larger0", tag="sheet7", align_bytes=64)
                take_max(0, slice(0, PACK), every)
            if s == 2:
                first = held.tile([P, PAIRS], F32, name="first_held", tag="w1_grouped_a", align_bytes=64)
            else:
                first = ring.tile([P, PAIRS], F32, name="first")
            nc.vector.tensor_copy(first[:], h[:].indirect(p1[:]))
            a1[s] = held.tile([P, PAIRS], F32, name=f"a1_{s}", tag=f"gained{s + 1}")
            nc.gpsimd.tensor_tensor(a1[s][:], first[:], second[:], ALU.subtract)
            nc.vector.tensor_copy(cards[b][:, t, :], h[:].indirect(p4[:]))
            if s == 7:
                grouped["card", 1] = interleave(cards[1], "card_grouped1", "card_grouped1")
            if s == 6:
                a2 = held.tile([P, PACK, KEPT], F32, name="a2")
                nc.gpsimd.tensor_tensor(a2[:], larger[0][:], cards[0][:], ALU.mult)
                grouped["a2", 0] = interleave(a2, "a2_grouped0", "a2_grouped0")
            if s + 2 < SLICES:
                hs.append(make_h(s + 2))
            if s > 0:
                nc.vector.tensor_copy(kept[(s - 1) // PACK][:, (s - 1) % PACK, :], a1[s - 1][:].indirect(p3[:]))
            if s in (0, 1):
                quantize_w1(nc.scalar.copy, s, 1, 0, PACK, ("w1_grouped_b", "w1_grouped_a")[s])
            if s == 5:
                grouped["card", 0] = interleave(cards[0], "card_grouped0", "sheet6")
                for c in range(R_PASSES):
                    tag = ("w1_grouped_b", "w1_grouped_a")[c]
                    w3_q[c] = quantize(interleave(w3_raw[c], f"w3_grouped{c}", tag), f"w3_{c}")
                card_passes(0, w3_q[0], quantize(grouped["card", 0], "card0"))
            if s == 6:
                codes, scales = quantize(grouped["a2", 0], "a2_0")
                for u in range(HALVES):
                    pair_passes(0, u, codes[:, halves[u]], scales[:, halves[u]])
        larger[1] = held.tile([P, PACK, KEPT], F32, name="larger1", tag="sheet7", align_bytes=64)
        take_max(1, slice(0, PACK - 1), every)
        card_passes(1, w3_q[1], quantize(grouped["card", 1], "card1"))
        last = PACK - 1
        for u in range(HALVES):
            nc.vector.tensor_copy(kept[1][:, last, halves[u]], a1[SLICES - 1][:].indirect(p3[:, u * HALF // 16 : (u + 1) * HALF // 16]))
        for u in range(HALVES):
            take_max(1, slice(last, PACK), halves[u])
        a2_last = []
        for u in range(HALVES):
            woven_a2 = held.tile([P, PACK * HALF], BF16, name=f"a2_grouped1{u}", align_bytes=64)
            nc.vector.tensor_tensor(
                woven(woven_a2), by_runs(larger[1][:, :, halves[u]]), by_runs(cards[1][:, :, halves[u]]), ALU.mult
            )
            a2_last.append(woven_a2)
        for u in range(HALVES):
            codes, scales = quantize(a2_last[u], f"a2_1{u}")
            pair_passes(1, u, codes[:], scales[:])

        out_rows = out.rearrange("(c p) j -> p c j", p=P)
        for u in range(HALVES):
            for c0 in range(0, N_TILES, 2):
                tiles = slice(c0, c0 + 2)
                squashed = held.tile([P, 2, HALF], F32, name=f"squashed{u}{c0}")
                nc.scalar.activation(squashed[:], y2[u][:, tiles, :], ACT.Tanh)
                scores = held.tile([P, 2, HALF], F32, name=f"scores{u}{c0}")
                nc.vector.tensor_tensor(
                    scores[:], squashed[:], out_gains[:, tiles].unsqueeze(2).to_broadcast([P, 2, HALF]), ALU.mult
                )
                nc.sync.dma_start(out=out_rows[:, tiles, halves[u]], in_=scores[:])
